import numpy as np
import ml_dtypes


def mxq(x, axis, fmt="e4m3"):
    dtype, down = {"e4m3": (ml_dtypes.float8_e4m3fn, 7), "e5m2": (ml_dtypes.float8_e5m2, 14)}[fmt]
    v = np.moveaxis(np.asarray(x, np.float32).astype(ml_dtypes.bfloat16).astype(np.float64), axis, -1)
    blocks = v.reshape(v.shape[:-1] + (-1, 32))
    amax = np.abs(blocks).max(-1, keepdims=True)
    byte = np.maximum(np.where(amax > 0, np.frexp(amax)[1] - 1 + 127, 0) - down, 1)
    scale = np.exp2(byte - 127.0)
    codes = (blocks / scale).astype(np.float32).astype(dtype).astype(np.float64)
    return np.moveaxis((codes * scale).reshape(v.shape), -1, axis)


WIDE = False


def mx_kscale(k):
    if not WIDE:
        return np.ones(k)
    levels = np.array([10, -10, 5, -5, 0])
    if k % 512:
        return np.exp2(np.random.permutation(np.resize(levels, k // 32))).repeat(32)
    a = np.empty((k // 512, 16))
    for p in range(k // 512):
        a[p, :8] = np.random.permutation(np.resize(levels, 8))
        for g in range(8):
            far = levels[np.abs(levels - a[p, g]) >= 10]
            a[p, g + 8] = far[np.random.randint(len(far))]
    return np.exp2(a.ravel()).repeat(32)


def f64(x):
    return np.asarray(x).astype(np.float64)


def striped(idx):
    return np.tile(idx.reshape(-1, 16).T, (8, 1)).astype(np.uint16)


def unstriped(offs):
    return offs[:16].T.reshape(-1).astype(np.int64)


E2M1 = np.array([0.0, 0.5, 1.0, 1.5, 2.0, 3.0, 4.0, 6.0, -0.0, -0.5, -1.0, -1.5, -2.0, -3.0, -4.0, -6.0])


def pack_weight(w, fmt):
    k, n = w.shape
    w = f64(np.asarray(w, np.float32).astype(ml_dtypes.bfloat16)).reshape(k // 32, 32, n)
    amax = np.abs(w).max(1)
    if fmt == "e4m3":
        byte = np.frexp(amax)[1] - 1 + 127 - 7
    else:
        mant, ex = np.frexp(amax / 6.0)
        byte = np.where(mant > 0.5, ex, ex - 1) + 127
    byte = np.clip(np.where(amax > 0, byte, 1), 1, 254)
    scaled = (w * np.exp2(127.0 - byte)[:, None, :]).reshape(k, n).astype(np.float32)
    by_word = np.ascontiguousarray(scaled.reshape(k // 512, 128, 4, n).transpose(0, 1, 3, 2))
    if fmt == "e4m3":
        words = by_word.astype(ml_dtypes.float8_e4m3fn).view(np.uint8)
    else:
        c = by_word.astype(ml_dtypes.float4_e2m1fn).view(np.uint8) & 0xF
        words = (c[..., 0::2] | (c[..., 1::2] << 4)).reshape(k // 512, 128, 2 * n)
    return np.ascontiguousarray(words), np.ascontiguousarray(byte.astype(np.uint8).reshape(k // 512, 16, n))


def unpack_weight(words, scales, fmt):
    g, _, n = scales.shape
    words = np.ascontiguousarray(words).reshape(g, 128, n, -1)
    if fmt == "e4m3":
        vals = words.view(ml_dtypes.float8_e4m3fn).astype(np.float64)
    else:
        nib = np.empty((g, 128, n, 4), np.uint8)
        nib[..., 0::2] = words & 0xF
        nib[..., 1::2] = words >> 4
        vals = E2M1[nib]
    vals = vals * np.repeat(np.exp2(scales.astype(np.float64) - 127.0), 8, axis=1)[..., None]
    return vals.transpose(0, 1, 3, 2).reshape(g * 512, n)


def planes(y):
    n, m = y.shape
    v = y.astype(np.float32).astype(ml_dtypes.bfloat16).astype(np.float64).reshape(n // 32, 32, m)
    top = np.abs(v).max(1)
    byte = np.clip(np.where(top > 0, np.frexp(top)[1] - 1 + 127 - 7, 1), 1, 254)
    codes = (v * np.exp2(127.0 - byte)[:, None, :]).reshape(n, m).astype(np.float32).astype(ml_dtypes.float8_e4m3fn).view(np.uint8)
    words = codes.reshape(n // 512, 128, 4, m).transpose(0, 1, 3, 2)
    return np.ascontiguousarray(words), np.ascontiguousarray(byte.astype(np.uint8).reshape(n // 512, 16, m))


def relu(v):
    return np.maximum(v, 0.0)


K, T, E, B, H, N = 1024, 768, 6, 4, 512, 512


def setup_inputs():
    n = np.random.standard_normal
    s = mx_kscale(K)
    u = mx_kscale(H)
    slot_token = np.random.permutation(T)[:128 * B]
    block = np.sort(np.random.randint(E, size=B))
    x = pack_weight(n((K, T)) * s[:, None], "e4m3")
    w = pack_weight(n((K, N)) / np.sqrt(K) / s[:, None], "e4m3")
    wa = pack_weight(n((K, E * H)) / np.sqrt(K) / s[:, None] * np.tile(u, E), "e4m3")
    wb = pack_weight(n((H, E * N)) / np.sqrt(H) / u[:, None], "e4m3")
    return {
        "x_words": x[0],
        "x_scales": x[1],
        "w_words": w[0],
        "w_scales": w[1],
        "wa_words": wa[0],
        "wa_scales": wa[1],
        "wb_words": wb[0],
        "wb_scales": wb[1],
        "gate": (np.tile(np.random.uniform(0.2, 1.0, 128 * B), (128, 1))).astype(np.float32),
        "offs": striped(slot_token),
        "offs2": striped((block[:, None] * H + np.arange(H)).reshape(-1)),
        "offs3": striped((block[:, None] * N + np.arange(N)).reshape(-1)),
    }


def reference(x_words, x_scales, w_words, w_scales, wa_words, wa_scales, wb_words, wb_scales, gate, offs, offs2, offs3):
    w = unpack_weight(w_words, w_scales, "e4m3")
    idx, idx2, idx3 = unstriped(offs), unstriped(offs2), unstriped(offs3)
    x = unpack_weight(x_words, x_scales, "e4m3")
    out = w.T @ x
    wa = unpack_weight(wa_words, wa_scales, "e4m3")[:, idx2]
    wb = unpack_weight(wb_words, wb_scales, "e4m3")[:, idx3]
    xq = x[:, idx]
    h = np.concatenate([wa[:, m * H:(m + 1) * H].T @ xq[:, 128 * m:128 * m + 128] for m in range(B)], axis=1)
    hq = mxq(relu(h), 0, "e4m3")
    y = np.concatenate([wb[:, m * N:(m + 1) * N].T @ hq[:, 128 * m:128 * m + 128] for m in range(B)], axis=1)
    out[:, idx] += f64(gate[:1]) * y
    out_0 = out
    return (out_0,) + planes(out_0)

@@ -1,0 +1,320 @@
+from contextlib import ExitStack
+
+import concourse.mybir as mybir
+from concourse.masks import make_identity
+
+K, T, E, B, H, N = 1024, 768, 6, 4, 512, 512
+FLOPS = 2 * K * N * T + 2 * (K * H + H * N) * 128 * B
+
+F32 = mybir.dt.float32
+BF16 = mybir.dt.bfloat16
+I32 = mybir.dt.int32
+U32 = mybir.dt.uint32
+U16 = mybir.dt.uint16
+U8 = mybir.dt.uint8
+FP8X4 = mybir.dt.float8_e4m3fn_x4
+COPY = mybir.ActivationFunctionType.Copy
+RELU = mybir.ActivationFunctionType.Relu
+ADD = mybir.AluOpType.add
+
+P = 128
+PACK = 4
+PASSES = K // (P * PACK)
+SLOTS = P * B
+POOL = E * H
+CHUNK = 256
+CHUNKS = T // CHUNK
+ALIGN = 64
+
+
+def tile_moe_dyl_relu_kernel(
+    tc, x_words, x_scales, w_words, w_scales, wa_words, wa_scales, wb_words, wb_scales,
+    gate, offs, offs2, offs3, out_0, out_1, out_2,
+):
+    nc = tc.nc
+    with ExitStack() as ctx:
+        sb = ctx.enter_context(tc.tile_pool(name="sb", bufs=1))
+        ps = ctx.enter_context(tc.psum_pool(name="ps", bufs=1))
+
+        def sbuf(shape, dtype, name, tag=None):
+            return sb.tile(shape, dtype, name=name, tag=tag or name, align_bytes=ALIGN)
+
+        def bank(name, tag):
+            return ps.tile([P, 512], F32, name=name, tag=tag)
+
+        def load_words(tile_ap, words):
+            nc.sync.dma_start(tile_ap.bitcast(I32), words.rearrange("p c d -> p (c d)").bitcast(I32))
+
+        def load_scales(plane, scales, queue):
+            rows = PACK * scales.shape[0]
+            for q in range(4):
+                queue.dma_start(
+                    plane[32 * q : 32 * q + rows, :].bitcast(I32),
+                    scales[:, 4 * q : 4 * q + 4, :].bitcast(I32),
+                )
+
+        tok_list = sb.tile([P, SLOTS // 16], U16, name="tok_list")
+        wa_list = sb.tile([P, B * H // 16], U16, name="wa_list")
+        wb_list = sb.tile([P, B * N // 16], U16, name="wb_list")
+        x_w = [sbuf([P, T], U32, "x_w%d" % a) for a in range(PASSES)]
+        x_s = sbuf([P, T], U8, "x_s")
+        wa_w = [sbuf([P, POOL], U32, "wa_w%d" % a) for a in range(PASSES)]
+        wa_s = sbuf([P, POOL], U8, "wa_s")
+        wb_w = sbuf([P, POOL], U32, "wb_w")
+        wb_s = sbuf([P, POOL], U8, "wb_s")
+        w_w = sbuf([P, PASSES, N], U32, "w_w")
+        w_s = sbuf([P, N], U8, "w_s")
+        gate_rows = sbuf([P, P], F32, "gate_rows")
+        ident = sbuf([P, P], F32, "ident")
+        routed = [sbuf([P, T], F32, "routed%d" % t) for t in range(PACK)]
+
+        wa_s_words = wa_s[:].bitcast(I32)
+        nc.vector.memset(wa_s_words[:, 0:448], 0)
+        nc.gpsimd.memset(gate_rows[:], 0.0)
+        nc.gpsimd.memset(wa_s_words[:, 448:], 0)
+        for plane in (x_s, w_s, wb_s):
+            nc.vector.memset(plane[:].bitcast(I32), 0)
+        make_identity(nc, ident[:])
+        for t in range(PACK):
+            (nc.vector if t == 0 else nc.gpsimd).memset(routed[t][:], 0.0)
+
+        nc.sync.dma_start(tok_list[:], offs)
+        nc.sync.dma_start(wa_list[:], offs2)
+        nc.sync.dma_start(wb_list[:], offs3)
+        load_words(x_w[0][:], x_words[0])
+        nc.sync.dma_start(gate_rows[0:B, :], gate[0:1, :].rearrange("o (m u) -> (o m) u", m=B))
+        load_words(x_w[1][:], x_words[1])
+        load_scales(wa_s, wa_scales, nc.sync)
+        nc.sync.dma_start(
+            w_w[:].bitcast(I32), w_words.rearrange("a p c d -> p a (c d)").bitcast(I32)
+        )
+        load_scales(x_s, x_scales, nc.sync)
+        load_scales(w_s, w_scales, nc.sync)
+        for a in range(PASSES):
+            load_words(wa_w[a][:], wa_words[a])
+        load_scales(wb_s, wb_scales, nc.sync)
+        load_words(wb_w[:], wb_words[0])
+
+        def gather(out, window, offsets, m, width):
+            cols = width // 16
+            nc.vector.tensor_copy(out, window[:].indirect(offsets[:, m * cols : (m + 1) * cols]))
+
+        def mx(out, lhs_w, lhs_s, rhs_w, rhs_s, a, passes):
+            nc.tensor.matmul_mx(
+                out=out, lhsT=lhs_w.bitcast(FP8X4), lhsT_scale=lhs_s, rhs=rhs_w.bitcast(FP8X4),
+                rhs_scale=rhs_s, start=(a == 0), stop=(a == passes - 1),
+            )
+
+        wp_w = sbuf([P, PASSES, PACK, P], U32, "wp_w")
+        wp_s = sbuf([P, PACK * P], U8, "wp_s")
+        for a in range(PASSES):
+            nc.scalar.copy(
+                wp_w[:, a].rearrange("p t (g i) -> p g t i", i=4),
+                w_w[:, a, :].rearrange("p (g i t) -> p g t i", i=4, t=PACK),
+            )
+        nc.gpsimd.tensor_copy(
+            wp_s[:].rearrange("p (t m) -> p t m", t=PACK), w_s[:].rearrange("p (m t) -> p t m", t=PACK)
+        )
+        base_tags = ("h_slots0", "h_slots1", "h_turn0", "h_turn1", "y_slots0", "y_slots1")
+        base = {}
+        for c in range(CHUNKS):
+            toks = slice(c * CHUNK, (c + 1) * CHUNK)
+            for half in range(2):
+                pair = bank("base%d_%d" % (c, half), base_tags[2 * c + half])
+                for t in (2 * half, 2 * half + 1):
+                    for a in range(PASSES):
+                        mx(pair[:, (t % 2) * CHUNK : (t % 2 + 1) * CHUNK], wp_w[:, a, t, :],
+                           wp_s[4 * a : P, t * P : (t + 1) * P], x_w[a][:, toks], x_s[4 * a : P, toks], a, PASSES)
+                held = sbuf([P, 2 * CHUNK], F32, "base_held%d_%d" % (c, half))
+                nc.scalar.copy(held[:], pair[:])
+                for t in (2 * half, 2 * half + 1):
+                    base[c, t] = held[:, (t % 2) * CHUNK : (t % 2 + 1) * CHUNK]
+
+        gate_bank = bank("gate_bank", "y_rows0")
+        nc.tensor.transpose(gate_bank[:, 0:P], gate_rows[:], ident[:])
+        gate_cols = sbuf([P, B], F32, "gate_cols")
+        nc.scalar.copy(gate_cols[:], gate_bank[:, 0:B])
+
+        xg_w = [sbuf([P, SLOTS], U32, "xg_w%d" % a) for a in range(PASSES)]
+        xg_s = sbuf([P, SLOTS], U8, "xg_s")
+        for a in range(PASSES):
+            gather(xg_w[a][:], x_w[a], tok_list, 0, SLOTS)
+
+        a_w, a_s, b_w, b_s = {}, {}, {}, {}
+        h_bank, h_pairs, h_turned, h_in, h_w, h_s = {}, {}, {}, {}, {}, {}
+        y_bank, y_turned, y_rows = {}, {}, {}
+
+        def gather_a_scales(m, tag=None):
+            a_s[m] = sbuf([P, H], U8, "a_s%d" % m, tag)
+            gather(a_s[m][:], wa_s, wa_list, m, H)
+
+        def gather_a_words(m, a, tag=None):
+            if a == 0:
+                a_w[m] = sbuf([P, PASSES, H], U32, "a_w%d" % m, tag)
+            gather(a_w[m][:, a, :], wa_w[a], wa_list, m, H)
+
+        def gather_b_scales(m, tag=None):
+            b_s[m] = sbuf([P, N], U8, "b_s%d" % m, tag)
+            gather(b_s[m][:], wb_s, wb_list, m, N)
+
+        def gather_b_words(m, tag=None):
+            b_w[m] = sbuf([P, N], U32, "b_w%d" % m, tag)
+            gather(b_w[m][:], wb_w, wb_list, m, N)
+
+        def h_product(m, tag):
+            h_bank[m] = bank("h_bank%d" % m, tag)
+            slots = slice(m * P, (m + 1) * P)
+            for a in range(PASSES):
+                mx(h_bank[m][:], xg_w[a][:, slots], xg_s[4 * a : P, slots],
+                   a_w[m][:, a, :], a_s[m][4 * a : P, :], a, PASSES)
+
+        def h_relu(m, tag=None):
+            h_pairs[m] = sbuf([P, H], BF16, "h_pairs%d" % m, tag)
+            nc.scalar.activation(
+                h_pairs[m][:].rearrange("s (u p e) -> s u p e", u=2, e=2),
+                h_bank[m][:].rearrange("s (p u e) -> s u p e", u=2, e=2), RELU,
+            )
+            h_turned[m] = bank("h_turned%d" % m, "h_turn%d" % (m % 2))
+            words = h_pairs[m][:].bitcast(F32)
+            for u in range(2):
+                nc.tensor.transpose(h_turned[m][:, u * P : (u + 1) * P], words[:, u * P : (u + 1) * P], ident[:])
+
+        def h_interleave(m, tag=None):
+            h_in[m] = sbuf([P, PACK * P], BF16, "h_in%d" % m, tag)
+            nc.scalar.copy(
+                h_in[m][:].bitcast(F32).rearrange("p (s u) -> p s u", u=2),
+                h_turned[m][:, 0 : 2 * P].rearrange("p (u s) -> p s u", u=2),
+            )
+
+        def h_quantize(m, tag=None):
+            h_w[m] = sbuf([P, P], U32, "h_w%d" % m, tag)
+            h_s[m] = sbuf([P, P], U8, "h_s%d" % m)
+            nc.vector.quantize_mx(out=h_w[m][:].bitcast(FP8X4), scales=h_s[m][:], in_=h_in[m][:])
+
+        def y_product(m, tag):
+            y_bank[m] = bank("y_bank%d" % m, tag)
+            mx(y_bank[m][:], h_w[m][:], h_s[m][:], b_w[m][:], b_s[m][:], 0, 1)
+
+        def y_gate(m, tags, tag=None):
+            gated = sbuf([P, PACK, P], F32, "gated%d" % m, tag)
+            nc.scalar.activation(
+                gated[:], y_bank[m][:].rearrange("s (p t) -> s t p", t=PACK), COPY, scale=gate_cols[:, m : m + 1],
+            )
+            for half in range(2):
+                if half == 0 or tags[1] != tags[0]:
+                    turned = bank("y_turned%d_%d" % (m, half), tags[half])
+                y_turned[m, half] = turned[:, half * 2 * P : (half + 1) * 2 * P]
+                for t in (2 * half, 2 * half + 1):
+                    nc.tensor.transpose(turned[:, t * P : (t + 1) * P], gated[:, t, :], ident[:])
+
+        def y_out(m, half, tag=None, on_vector=False):
+            y_rows[m, half] = sbuf([P, 2 * P], F32, "y_rows%d_%d" % (m, half), tag)
+            (nc.vector.tensor_copy if on_vector else nc.scalar.copy)(y_rows[m, half][:], y_turned[m, half])
+
+        def scatter(m, t, on_vector=False):
+            window = routed[t][:].indirect(tok_list[:, m * P // 16 : (m + 1) * P // 16])
+            values = y_rows[m, t // 2][:, (t % 2) * P : (t % 2 + 1) * P]
+            if on_vector:
+                nc.vector.tensor_copy(window, values)
+            else:
+                nc.scalar.activation(window, values, COPY)
+
+        for m in (0, 1, 2):
+            gather_a_scales(m)
+        gather(xg_s[:], x_s, tok_list, 0, SLOTS)
+        for m in (0, 1, 2):
+            gather_a_words(m, 0)
+        for m in (0, 1, 2):
+            gather_a_words(m, 1)
+            h_product(m, "h_slots%d" % (m % 2))
+            h_relu(m)
+            h_interleave(m)
+        gather_b_scales(0)
+        h_quantize(0)
+        gather_b_words(0)
+        y_product(0, "y_slots0")
+        y_gate(0, ("y_rows0", "y_rows0"))
+        gather_b_scales(1, "h_in0")
+        h_quantize(1)
+        gather_b_words(1)
+        y_product(1, "y_slots0")
+        y_out(0, 0)
+        y_out(0, 1)
+        y_gate(1, ("y_rows1", "y_rows1"))
+        gather_a_scales(3, "b_s0")
+        for a in range(PASSES):
+            gather_a_words(3, a, "b_w0")
+        h_product(3, "y_slots0")
+        for t in (0, 1):
+            scatter(0, t)
+        y_out(1, 0)
+        scatter(0, 2)
+        h_relu(3, "y_rows0_0")
+        y_out(1, 1)
+        scatter(0, 3)
+        h_interleave(3)
+        gather_b_scales(2, "h_in0")
+        h_quantize(2)
+        gather_b_words(2, "b_w1")
+        y_product(2, "y_slots1")
+        scatter(1, 0)
+        y_gate(2, ("y_rows0", "y_rows0"), "y_rows0_1")
+        scatter(1, 1)
+        scatter(1, 2)
+        gather_b_scales(3, "b_s0")
+        gather_b_words(3, "b_w1")
+        h_quantize(3)
+        y_product(3, "y_slots1")
+        y_out(2, 0)
+        y_out(2, 1)
+        y_gate(3, ("y_rows1", "y_slots0"), "y_rows1_0")
+        scatter(1, 3, on_vector=True)
+        scatter(2, 0)
+        scatter(2, 2, on_vector=True)
+        scatter(2, 3, on_vector=True)
+        scatter(2, 1)
+        y_out(3, 0, on_vector=True)
+        y_out(3, 1)
+        for t in range(PACK):
+            scatter(3, t, on_vector=t == 0)
+
+        out_rows = out_0.rearrange("(p t) j -> p t j", t=PACK)
+        out_words = out_1[0].rearrange("p j d -> p (j d)").bitcast(I32)
+        total = [sbuf([P, PACK, CHUNK], F32, "total%d" % c) for c in range(CHUNKS)]
+        o_s = sbuf([P, T], U8, "o_s")
+
+        def add(c, t):
+            nc.vector.tensor_tensor(total[c][:, t, :], base[c, t], routed[t][:, c * CHUNK : (c + 1) * CHUNK], ADD)
+
+        def store_half(c, half):
+            nc.sync.dma_start(
+                out_rows[:, 2 * half : 2 * half + 2, c * CHUNK : (c + 1) * CHUNK],
+                total[c][:, 2 * half : 2 * half + 2, :],
+            )
+
+        for t in (0, 1):
+            for c in range(CHUNKS):
+                add(c, t)
+                if t == 1:
+                    store_half(c, 0)
+        rounded = {}
+        for c in range(CHUNKS):
+            add(c, 2)
+            add(c, 3)
+            store_half(c, 1)
+            rounded[c] = sbuf([P, CHUNK * PACK], BF16, "rounded%d" % c)
+            dst = rounded[c][:].rearrange("p (g i t) -> p g t i", i=4, t=PACK)
+            src = total[c][:].rearrange("p t (g i) -> p g t i", i=4)
+            if c < CHUNKS - 1:
+                nc.scalar.copy(dst, src)
+            else:
+                nc.vector.tensor_copy(dst, src)
+        for c in range(CHUNKS):
+            o_w = sbuf([P, CHUNK], U32, "o_w%d" % c)
+            toks = slice(c * CHUNK, (c + 1) * CHUNK)
+            nc.vector.quantize_mx(out=o_w[:].bitcast(FP8X4), scales=o_s[:, toks], in_=rounded[c][:])
+            nc.sync.dma_start(out_words[:, toks], o_w[:].bitcast(I32))
+        for q in range(4):
+            (nc.sync if q % 2 else nc.scalar).dma_start(
+                out_2[0, 4 * q : 4 * q + 4, :].bitcast(I32), o_s[32 * q : 32 * q + 4, :].bitcast(I32)
+            )

@@ -16,6 +16,7 @@ FP8X4 = mybir.dt.float8_e4m3fn_x4
 COPY = mybir.ActivationFunctionType.Copy
 RELU = mybir.ActivationFunctionType.Relu
 ADD = mybir.AluOpType.add
+MULT = mybir.AluOpType.mult
 
 P = 128
 PACK = 4
@@ -149,9 +150,8 @@ def tile_moe_dyl_relu_kernel(
             gather(a_s[m][:], wa_s, wa_list, m, H)
 
         def gather_a_words(m, a, tag=None):
-            if a == 0:
-                a_w[m] = sbuf([P, PASSES, H], U32, "a_w%d" % m, tag)
-            gather(a_w[m][:, a, :], wa_w[a], wa_list, m, H)
+            a_w[m, a] = sbuf([P, H], U32, "a_w%d_%d" % (m, a), tag)
+            gather(a_w[m, a][:], wa_w[a], wa_list, m, H)
 
         def gather_b_scales(m, tag=None):
             b_s[m] = sbuf([P, N], U8, "b_s%d" % m, tag)
@@ -166,7 +166,7 @@ def tile_moe_dyl_relu_kernel(
             slots = slice(m * P, (m + 1) * P)
             for a in range(PASSES):
                 mx(h_bank[m][:], xg_w[a][:, slots], xg_s[4 * a : P, slots],
-                   a_w[m][:, a, :], a_s[m][4 * a : P, :], a, PASSES)
+                   a_w[m, a][:], a_s[m][4 * a : P, :], a, PASSES)
 
         def h_relu(m, tag=None):
             h_pairs[m] = sbuf([P, H], BF16, "h_pairs%d" % m, tag)
@@ -195,11 +195,13 @@ def tile_moe_dyl_relu_kernel(
             y_bank[m] = bank("y_bank%d" % m, tag)
             mx(y_bank[m][:], h_w[m][:], h_s[m][:], b_w[m][:], b_s[m][:], 0, 1)
 
-        def y_gate(m, tags, tag=None):
+        def y_gate(m, tags, tag=None, on_vector=False):
             gated = sbuf([P, PACK, P], F32, "gated%d" % m, tag)
-            nc.scalar.activation(
-                gated[:], y_bank[m][:].rearrange("s (p t) -> s t p", t=PACK), COPY, scale=gate_cols[:, m : m + 1],
-            )
+            dealt = y_bank[m][:].rearrange("s (p t) -> s t p", t=PACK)
+            if on_vector:
+                nc.vector.tensor_scalar(gated[:], dealt, gate_cols[:, m : m + 1], None, MULT)
+            else:
+                nc.scalar.activation(gated[:], dealt, COPY, scale=gate_cols[:, m : m + 1])
             for half in range(2):
                 if half == 0 or tags[1] != tags[0]:
                     turned = bank("y_turned%d_%d" % (m, half), tags[half])
@@ -207,76 +209,69 @@ def tile_moe_dyl_relu_kernel(
                 for t in (2 * half, 2 * half + 1):
                     nc.tensor.transpose(turned[:, t * P : (t + 1) * P], gated[:, t, :], ident[:])
 
-        def y_out(m, half, tag=None, on_vector=False):
-            y_rows[m, half] = sbuf([P, 2 * P], F32, "y_rows%d_%d" % (m, half), tag)
-            (nc.vector.tensor_copy if on_vector else nc.scalar.copy)(y_rows[m, half][:], y_turned[m, half])
+        def y_out(m, ts, tag=None, on_vector=False):
+            rows = sbuf([P, len(ts) * P], F32, "y_rows%d_%d" % (m, ts[0]), tag)
+            first = (ts[0] % 2) * P
+            (nc.vector.tensor_copy if on_vector else nc.scalar.copy)(
+                rows[:], y_turned[m, ts[0] // 2][:, first : first + len(ts) * P]
+            )
+            for i, t in enumerate(ts):
+                y_rows[m, t] = rows[:, i * P : (i + 1) * P]
 
         def scatter(m, t, on_vector=False):
             window = routed[t][:].indirect(tok_list[:, m * P // 16 : (m + 1) * P // 16])
-            values = y_rows[m, t // 2][:, (t % 2) * P : (t % 2 + 1) * P]
             if on_vector:
-                nc.vector.tensor_copy(window, values)
+                nc.vector.tensor_copy(window, y_rows[m, t])
             else:
-                nc.scalar.activation(window, values, COPY)
+                nc.scalar.activation(window, y_rows[m, t], COPY)
 
-        for m in (0, 1, 2):
+        for m in range(B):
             gather_a_scales(m)
         gather(xg_s[:], x_s, tok_list, 0, SLOTS)
-        for m in (0, 1, 2):
+        for m in range(B):
             gather_a_words(m, 0)
-        for m in (0, 1, 2):
+        for m in range(B):
             gather_a_words(m, 1)
             h_product(m, "h_slots%d" % (m % 2))
             h_relu(m)
             h_interleave(m)
-        gather_b_scales(0)
-        h_quantize(0)
-        gather_b_words(0)
-        y_product(0, "y_slots0")
-        y_gate(0, ("y_rows0", "y_rows0"))
-        gather_b_scales(1, "h_in0")
-        h_quantize(1)
-        gather_b_words(1)
-        y_product(1, "y_slots0")
-        y_out(0, 0)
-        y_out(0, 1)
-        y_gate(1, ("y_rows1", "y_rows1"))
-        gather_a_scales(3, "b_s0")
-        for a in range(PASSES):
-            gather_a_words(3, a, "b_w0")
-        h_product(3, "y_slots0")
-        for t in (0, 1):
-            scatter(0, t)
-        y_out(1, 0)
+        gather_b_scales(0, "b_s")
+        gather_b_words(0, "b_w0")
+        for m in range(B):
+            if m > 0:
+                gather_b_scales(m, "b_s")
+            h_quantize(m, "h_w")
+            y_product(m, ("y_slots0", "y_slots0", "y_slots0", "y_slots1")[m])
+            if m < 2:
+                y_gate(m, ("y_rows%d" % m,) * 2)
+            if m + 1 < B:
+                gather_b_words(m + 1, "b_w%d" % ((m + 1) % 2))
+        y_out(0, (0, 1))
+        scatter(0, 0)
+        scatter(0, 1)
+        y_out(1, (0, 1))
+        y_out(1, (2, 3))
+        y_out(0, (2, 3), "gated1")
+        y_gate(2, ("y_rows0", "y_rows0"), "y_rows0_0")
         scatter(0, 2)
-        h_relu(3, "y_rows0_0")
-        y_out(1, 1)
         scatter(0, 3)
-        h_interleave(3)
-        gather_b_scales(2, "h_in0")
-        h_quantize(2)
-        gather_b_words(2, "b_w1")
-        y_product(2, "y_slots1")
-        scatter(1, 0)
-        y_gate(2, ("y_rows0", "y_rows0"), "y_rows0_1")
-        scatter(1, 1)
-        scatter(1, 2)
-        gather_b_scales(3, "b_s0")
-        gather_b_words(3, "b_w1")
-        h_quantize(3)
-        y_product(3, "y_slots1")
-        y_out(2, 0)
-        y_out(2, 1)
-        y_gate(3, ("y_rows1", "y_slots0"), "y_rows1_0")
-        scatter(1, 3, on_vector=True)
+        scatter(1, 0, on_vector=True)
+        scatter(1, 1, on_vector=True)
+        y_gate(3, ("h_slots0", "h_slots1"), on_vector=True)
+        scatter(1, 2, on_vector=True)
+        y_out(2, (0, 1))
         scatter(2, 0)
-        scatter(2, 2, on_vector=True)
-        scatter(2, 3, on_vector=True)
         scatter(2, 1)
-        y_out(3, 0, on_vector=True)
-        y_out(3, 1)
-        for t in range(PACK):
-            scatter(3, t, on_vector=t == 0)
+        y_out(3, (0, 1), on_vector=True)
+        scatter(1, 3, on_vector=True)
+        y_out(2, (2, 3))
+        scatter(3, 0, on_vector=True)
+        scatter(2, 3, on_vector=True)
+        y_out(3, (2, 3))
+        scatter(3, 1)
+        scatter(2, 2)
+        scatter(3, 2)
+        scatter(3, 3)
 
         out_rows = out_0.rearrange("(p t) j -> p t j", t=PACK)
         out_words = out_1[0].rearrange("p j d -> p (j d)").bitcast(I32)

@@ -77,22 +77,22 @@ def tile_moe_dyl_relu_kernel(
             nc.vector.memset(plane[:].bitcast(I32), 0)
         make_identity(nc, ident[:])
         for t in range(PACK):
-            (nc.vector if t == 0 else nc.gpsimd).memset(routed[t][:], 0.0)
+            nc.vector.memset(routed[t][:].bitcast(I32), 0)
 
+        load_words(x_w[0][:], x_words[0])
         nc.sync.dma_start(tok_list[:], offs)
         nc.sync.dma_start(wa_list[:], offs2)
         nc.sync.dma_start(wb_list[:], offs3)
-        load_words(x_w[0][:], x_words[0])
         nc.sync.dma_start(gate_rows[0:B, :], gate[0:1, :].rearrange("o (m u) -> (o m) u", m=B))
         load_words(x_w[1][:], x_words[1])
         load_scales(wa_s, wa_scales, nc.sync)
+        load_words(wa_w[0][:], wa_words[0])
+        load_scales(x_s, x_scales, nc.sync)
         nc.sync.dma_start(
             w_w[:].bitcast(I32), w_words.rearrange("a p c d -> p a (c d)").bitcast(I32)
         )
-        load_scales(x_s, x_scales, nc.sync)
         load_scales(w_s, w_scales, nc.sync)
-        for a in range(PASSES):
-            load_words(wa_w[a][:], wa_words[a])
+        load_words(wa_w[1][:], wa_words[1])
         load_scales(wb_s, wb_scales, nc.sync)
         load_words(wb_w[:], wb_words[0])
 
@@ -239,7 +239,7 @@ def tile_moe_dyl_relu_kernel(
         gather_b_words(0, "b_w0")
         for m in range(B):
             if m > 0:
-                gather_b_scales(m, "b_s")
+                gather_b_scales(m, "b_s" if m == 1 else "h_in%d" % (m - 1))
             h_quantize(m, "h_w")
             y_product(m, ("y_slots0", "y_slots0", "y_slots0", "y_slots1")[m])
             if m < 2:

from contextlib import ExitStack

import concourse.mybir as mybir
from concourse.masks import make_identity

K, T, E, B, H, N = 1024, 768, 6, 4, 512, 512
FLOPS = 2 * K * N * T + 2 * (K * H + H * N) * 128 * B

F32 = mybir.dt.float32
BF16 = mybir.dt.bfloat16
I32 = mybir.dt.int32
U32 = mybir.dt.uint32
U16 = mybir.dt.uint16
U8 = mybir.dt.uint8
FP8X4 = mybir.dt.float8_e4m3fn_x4
COPY = mybir.ActivationFunctionType.Copy
RELU = mybir.ActivationFunctionType.Relu
ADD = mybir.AluOpType.add
MULT = mybir.AluOpType.mult

P = 128
PACK = 4
PASSES = K // (P * PACK)
SLOTS = P * B
POOL = E * H
CHUNK = 256
CHUNKS = T // CHUNK
ALIGN = 64


def tile_moe_dyl_relu_kernel(
    tc, x_words, x_scales, w_words, w_scales, wa_words, wa_scales, wb_words, wb_scales,
    gate, offs, offs2, offs3, out_0, out_1, out_2,
):
    nc = tc.nc
    with ExitStack() as ctx:
        sb = ctx.enter_context(tc.tile_pool(name="sb", bufs=1))
        ps = ctx.enter_context(tc.psum_pool(name="ps", bufs=1))

        def sbuf(shape, dtype, name, tag=None):
            return sb.tile(shape, dtype, name=name, tag=tag or name, align_bytes=ALIGN)

        def bank(name, tag):
            return ps.tile([P, 512], F32, name=name, tag=tag)

        def load_words(tile_ap, words):
            nc.sync.dma_start(tile_ap.bitcast(I32), words.rearrange("p c d -> p (c d)").bitcast(I32))

        def load_scales(plane, scales, queue):
            rows = PACK * scales.shape[0]
            for q in range(4):
                queue.dma_start(
                    plane[32 * q : 32 * q + rows, :].bitcast(I32),
                    scales[:, 4 * q : 4 * q + 4, :].bitcast(I32),
                )

        tok_list = sb.tile([P, SLOTS // 16], U16, name="tok_list")
        wa_list = sb.tile([P, B * H // 16], U16, name="wa_list")
        wb_list = sb.tile([P, B * N // 16], U16, name="wb_list")
        x_w = [sbuf([P, T], U32, "x_w%d" % a) for a in range(PASSES)]
        x_s = sbuf([P, T], U8, "x_s")
        wa_w = [sbuf([P, POOL], U32, "wa_w%d" % a) for a in range(PASSES)]
        wa_s = sbuf([P, POOL], U8, "wa_s")
        wb_w = sbuf([P, POOL], U32, "wb_w")
        wb_s = sbuf([P, POOL], U8, "wb_s")
        w_w = sbuf([P, PASSES, N], U32, "w_w")
        w_s = sbuf([P, N], U8, "w_s")
        gate_rows = sbuf([P, P], F32, "gate_rows")
        ident = sbuf([P, P], F32, "ident")
        routed = [sbuf([P, T], F32, "routed%d" % t) for t in range(PACK)]

        wa_s_words = wa_s[:].bitcast(I32)
        nc.vector.memset(wa_s_words[:, 0:448], 0)
        nc.gpsimd.memset(gate_rows[:], 0.0)
        nc.gpsimd.memset(wa_s_words[:, 448:], 0)
        for plane in (x_s, w_s, wb_s):
            nc.vector.memset(plane[:].bitcast(I32), 0)
        make_identity(nc, ident[:])
        for t in range(PACK):
            nc.vector.memset(routed[t][:].bitcast(I32), 0)

        load_words(x_w[0][:], x_words[0])
        nc.sync.dma_start(tok_list[:], offs)
        nc.sync.dma_start(wa_list[:], offs2)
        nc.sync.dma_start(wb_list[:], offs3)
        nc.sync.dma_start(gate_rows[0:B, :], gate[0:1, :].rearrange("o (m u) -> (o m) u", m=B))
        load_words(x_w[1][:], x_words[1])
        load_scales(wa_s, wa_scales, nc.sync)
        load_words(wa_w[0][:], wa_words[0])
        load_scales(x_s, x_scales, nc.sync)
        nc.sync.dma_start(
            w_w[:].bitcast(I32), w_words.rearrange("a p c d -> p a (c d)").bitcast(I32)
        )
        load_scales(w_s, w_scales, nc.sync)
        load_words(wa_w[1][:], wa_words[1])
        load_scales(wb_s, wb_scales, nc.sync)
        load_words(wb_w[:], wb_words[0])

        def gather(out, window, offsets, m, width):
            cols = width // 16
            nc.vector.tensor_copy(out, window[:].indirect(offsets[:, m * cols : (m + 1) * cols]))

        def mx(out, lhs_w, lhs_s, rhs_w, rhs_s, a, passes):
            nc.tensor.matmul_mx(
                out=out, lhsT=lhs_w.bitcast(FP8X4), lhsT_scale=lhs_s, rhs=rhs_w.bitcast(FP8X4),
                rhs_scale=rhs_s, start=(a == 0), stop=(a == passes - 1),
            )

        wp_w = sbuf([P, PASSES, PACK, P], U32, "wp_w")
        wp_s = sbuf([P, PACK * P], U8, "wp_s")
        for a in range(PASSES):
            nc.scalar.copy(
                wp_w[:, a].rearrange("p t (g i) -> p g t i", i=4),
                w_w[:, a, :].rearrange("p (g i t) -> p g t i", i=4, t=PACK),
            )
        nc.gpsimd.tensor_copy(
            wp_s[:].rearrange("p (t m) -> p t m", t=PACK), w_s[:].rearrange("p (m t) -> p t m", t=PACK)
        )
        base_tags = ("h_slots0", "h_slots1", "h_turn0", "h_turn1", "y_slots0", "y_slots1")
        base = {}
        for c in range(CHUNKS):
            toks = slice(c * CHUNK, (c + 1) * CHUNK)
            for half in range(2):
                pair = bank("base%d_%d" % (c, half), base_tags[2 * c + half])
                for t in (2 * half, 2 * half + 1):
                    for a in range(PASSES):
                        mx(pair[:, (t % 2) * CHUNK : (t % 2 + 1) * CHUNK], wp_w[:, a, t, :],
                           wp_s[4 * a : P, t * P : (t + 1) * P], x_w[a][:, toks], x_s[4 * a : P, toks], a, PASSES)
                held = sbuf([P, 2 * CHUNK], F32, "base_held%d_%d" % (c, half))
                nc.scalar.copy(held[:], pair[:])
                for t in (2 * half, 2 * half + 1):
                    base[c, t] = held[:, (t % 2) * CHUNK : (t % 2 + 1) * CHUNK]

        gate_bank = bank("gate_bank", "y_rows0")
        nc.tensor.transpose(gate_bank[:, 0:P], gate_rows[:], ident[:])
        gate_cols = sbuf([P, B], F32, "gate_cols")
        nc.scalar.copy(gate_cols[:], gate_bank[:, 0:B])

        xg_w = [sbuf([P, SLOTS], U32, "xg_w%d" % a) for a in range(PASSES)]
        xg_s = sbuf([P, SLOTS], U8, "xg_s")
        for a in range(PASSES):
            gather(xg_w[a][:], x_w[a], tok_list, 0, SLOTS)

        a_w, a_s, b_w, b_s = {}, {}, {}, {}
        h_bank, h_pairs, h_turned, h_in, h_w, h_s = {}, {}, {}, {}, {}, {}
        y_bank, y_turned, y_rows = {}, {}, {}

        def gather_a_scales(m, tag=None):
            a_s[m] = sbuf([P, H], U8, "a_s%d" % m, tag)
            gather(a_s[m][:], wa_s, wa_list, m, H)

        def gather_a_words(m, a, tag=None):
            a_w[m, a] = sbuf([P, H], U32, "a_w%d_%d" % (m, a), tag)
            gather(a_w[m, a][:], wa_w[a], wa_list, m, H)

        def gather_b_scales(m, tag=None):
            b_s[m] = sbuf([P, N], U8, "b_s%d" % m, tag)
            gather(b_s[m][:], wb_s, wb_list, m, N)

        def gather_b_words(m, tag=None):
            b_w[m] = sbuf([P, N], U32, "b_w%d" % m, tag)
            gather(b_w[m][:], wb_w, wb_list, m, N)

        def h_product(m, tag):
            h_bank[m] = bank("h_bank%d" % m, tag)
            slots = slice(m * P, (m + 1) * P)
            for a in range(PASSES):
                mx(h_bank[m][:], xg_w[a][:, slots], xg_s[4 * a : P, slots],
                   a_w[m, a][:], a_s[m][4 * a : P, :], a, PASSES)

        def h_relu(m, tag=None):
            h_pairs[m] = sbuf([P, H], BF16, "h_pairs%d" % m, tag)
            nc.scalar.activation(
                h_pairs[m][:].rearrange("s (u p e) -> s u p e", u=2, e=2),
                h_bank[m][:].rearrange("s (p u e) -> s u p e", u=2, e=2), RELU,
            )
            h_turned[m] = bank("h_turned%d" % m, "h_turn%d" % (m % 2))
            words = h_pairs[m][:].bitcast(F32)
            for u in range(2):
                nc.tensor.transpose(h_turned[m][:, u * P : (u + 1) * P], words[:, u * P : (u + 1) * P], ident[:])

        def h_interleave(m, tag=None):
            h_in[m] = sbuf([P, PACK * P], BF16, "h_in%d" % m, tag)
            nc.scalar.copy(
                h_in[m][:].bitcast(F32).rearrange("p (s u) -> p s u", u=2),
                h_turned[m][:, 0 : 2 * P].rearrange("p (u s) -> p s u", u=2),
            )

        def h_quantize(m, tag=None):
            h_w[m] = sbuf([P, P], U32, "h_w%d" % m, tag)
            h_s[m] = sbuf([P, P], U8, "h_s%d" % m)
            nc.vector.quantize_mx(out=h_w[m][:].bitcast(FP8X4), scales=h_s[m][:], in_=h_in[m][:])

        def y_product(m, tag):
            y_bank[m] = bank("y_bank%d" % m, tag)
            mx(y_bank[m][:], h_w[m][:], h_s[m][:], b_w[m][:], b_s[m][:], 0, 1)

        def y_gate(m, tags, tag=None, on_vector=False):
            gated = sbuf([P, PACK, P], F32, "gated%d" % m, tag)
            dealt = y_bank[m][:].rearrange("s (p t) -> s t p", t=PACK)
            if on_vector:
                nc.vector.tensor_scalar(gated[:], dealt, gate_cols[:, m : m + 1], None, MULT)
            else:
                nc.scalar.activation(gated[:], dealt, COPY, scale=gate_cols[:, m : m + 1])
            for half in range(2):
                if half == 0 or tags[1] != tags[0]:
                    turned = bank("y_turned%d_%d" % (m, half), tags[half])
                y_turned[m, half] = turned[:, half * 2 * P : (half + 1) * 2 * P]
                for t in (2 * half, 2 * half + 1):
                    nc.tensor.transpose(turned[:, t * P : (t + 1) * P], gated[:, t, :], ident[:])

        def y_out(m, ts, tag=None, on_vector=False):
            rows = sbuf([P, len(ts) * P], F32, "y_rows%d_%d" % (m, ts[0]), tag)
            first = (ts[0] % 2) * P
            (nc.vector.tensor_copy if on_vector else nc.scalar.copy)(
                rows[:], y_turned[m, ts[0] // 2][:, first : first + len(ts) * P]
            )
            for i, t in enumerate(ts):
                y_rows[m, t] = rows[:, i * P : (i + 1) * P]

        def scatter(m, t, on_vector=False):
            window = routed[t][:].indirect(tok_list[:, m * P // 16 : (m + 1) * P // 16])
            if on_vector:
                nc.vector.tensor_copy(window, y_rows[m, t])
            else:
                nc.scalar.activation(window, y_rows[m, t], COPY)

        for m in range(B):
            gather_a_scales(m)
        gather(xg_s[:], x_s, tok_list, 0, SLOTS)
        for m in range(B):
            gather_a_words(m, 0)
        for m in range(B):
            gather_a_words(m, 1)
            h_product(m, "h_slots%d" % (m % 2))
            h_relu(m)
            h_interleave(m)
        gather_b_scales(0, "b_s")
        gather_b_words(0, "b_w0")
        for m in range(B):
            if m > 0:
                gather_b_scales(m, "b_s" if m == 1 else "h_in%d" % (m - 1))
            h_quantize(m, "h_w")
            y_product(m, ("y_slots0", "y_slots0", "y_slots0", "y_slots1")[m])
            if m < 2:
                y_gate(m, ("y_rows%d" % m,) * 2)
            if m + 1 < B:
                gather_b_words(m + 1, "b_w%d" % ((m + 1) % 2))
        y_out(0, (0, 1))
        scatter(0, 0)
        scatter(0, 1)
        y_out(1, (0, 1))
        y_out(1, (2, 3))
        y_out(0, (2, 3), "gated1")
        y_gate(2, ("y_rows0", "y_rows0"), "y_rows0_0")
        scatter(0, 2)
        scatter(0, 3)
        scatter(1, 0, on_vector=True)
        scatter(1, 1, on_vector=True)
        y_gate(3, ("h_slots0", "h_slots1"), on_vector=True)
        scatter(1, 2, on_vector=True)
        y_out(2, (0, 1))
        scatter(2, 0)
        scatter(2, 1)
        y_out(3, (0, 1), on_vector=True)
        scatter(1, 3, on_vector=True)
        y_out(2, (2, 3))
        scatter(3, 0, on_vector=True)
        scatter(2, 3, on_vector=True)
        y_out(3, (2, 3))
        scatter(3, 1)
        scatter(2, 2)
        scatter(3, 2)
        scatter(3, 3)

        out_rows = out_0.rearrange("(p t) j -> p t j", t=PACK)
        out_words = out_1[0].rearrange("p j d -> p (j d)").bitcast(I32)
        total = [sbuf([P, PACK, CHUNK], F32, "total%d" % c) for c in range(CHUNKS)]
        o_s = sbuf([P, T], U8, "o_s")

        def add(c, t):
            nc.vector.tensor_tensor(total[c][:, t, :], base[c, t], routed[t][:, c * CHUNK : (c + 1) * CHUNK], ADD)

        def store_half(c, half):
            nc.sync.dma_start(
                out_rows[:, 2 * half : 2 * half + 2, c * CHUNK : (c + 1) * CHUNK],
                total[c][:, 2 * half : 2 * half + 2, :],
            )

        for t in (0, 1):
            for c in range(CHUNKS):
                add(c, t)
                if t == 1:
                    store_half(c, 0)
        rounded = {}
        for c in range(CHUNKS):
            add(c, 2)
            add(c, 3)
            store_half(c, 1)
            rounded[c] = sbuf([P, CHUNK * PACK], BF16, "rounded%d" % c)
            dst = rounded[c][:].rearrange("p (g i t) -> p g t i", i=4, t=PACK)
            src = total[c][:].rearrange("p t (g i) -> p g t i", i=4)
            if c < CHUNKS - 1:
                nc.scalar.copy(dst, src)
            else:
                nc.vector.tensor_copy(dst, src)
        for c in range(CHUNKS):
            o_w = sbuf([P, CHUNK], U32, "o_w%d" % c)
            toks = slice(c * CHUNK, (c + 1) * CHUNK)
            nc.vector.quantize_mx(out=o_w[:].bitcast(FP8X4), scales=o_s[:, toks], in_=rounded[c][:])
            nc.sync.dma_start(out_words[:, toks], o_w[:].bitcast(I32))
        for q in range(4):
            (nc.sync if q % 2 else nc.scalar).dma_start(
                out_2[0, 4 * q : 4 * q + 4, :].bitcast(I32), o_s[32 * q : 32 * q + 4, :].bitcast(I32)
            )
